import numpy as np
import ml_dtypes


def mxq(x, axis, fmt="e4m3"):
    dtype, down = {"e4m3": (ml_dtypes.float8_e4m3fn, 7), "e5m2": (ml_dtypes.float8_e5m2, 14)}[fmt]
    v = np.moveaxis(np.asarray(x, np.float32).astype(ml_dtypes.bfloat16).astype(np.float64), axis, -1)
    blocks = v.reshape(v.shape[:-1] + (-1, 32))
    amax = np.abs(blocks).max(-1, keepdims=True)
    byte = np.maximum(np.where(amax > 0, np.frexp(amax)[1] - 1 + 127, 0) - down, 1)
    scale = np.exp2(byte - 127.0)
    codes = (blocks / scale).astype(np.float32).astype(dtype).astype(np.float64)
    return np.moveaxis((codes * scale).reshape(v.shape), -1, axis)


WIDE = False


def mx_kscale(k):
    if not WIDE:
        return np.ones(k)
    levels = np.array([10, -10, 5, -5, 0])
    if k % 512:
        return np.exp2(np.random.permutation(np.resize(levels, k // 32))).repeat(32)
    a = np.empty((k // 512, 16))
    for p in range(k // 512):
        a[p, :8] = np.random.permutation(np.resize(levels, 8))
        for g in range(8):
            far = levels[np.abs(levels - a[p, g]) >= 10]
            a[p, g + 8] = far[np.random.randint(len(far))]
    return np.exp2(a.ravel()).repeat(32)


def f64(x):
    return np.asarray(x).astype(np.float64)


def striped(idx):
    return np.tile(idx.reshape(-1, 16).T, (8, 1)).astype(np.uint16)


def unstriped(offs):
    return offs[:16].T.reshape(-1).astype(np.int64)


def striped8(idx):
    return np.concatenate([x.reshape(-1, 16).T for x in idx]).astype(np.uint16)


def runs(offs, k):
    lists = np.stack([offs[16 * r : 16 * r + 16].T.reshape(-1) for r in range(8)]).astype(np.int64)
    return lists[np.arange(k) % 512 // 64]


def pack_weight(w):
    k, n = w.shape
    w = f64(np.asarray(w, np.float32).astype(ml_dtypes.bfloat16)).reshape(k // 32, 32, n)
    amax = np.abs(w).max(1)
    byte = np.clip(np.where(amax > 0, np.frexp(amax)[1] - 1 + 127 - 7, 1), 1, 254)
    scaled = (w * np.exp2(127.0 - byte)[:, None, :]).reshape(k, n).astype(np.float32)
    words = np.ascontiguousarray(scaled.reshape(k // 512, 128, 4, n).transpose(0, 1, 3, 2)).astype(ml_dtypes.float8_e4m3fn).view(np.uint8)
    return words, np.ascontiguousarray(byte.astype(np.uint8).reshape(k // 512, 16, n))


def unpack_weight(words, scales):
    g, p, n, _ = words.shape
    vals = np.ascontiguousarray(words).view(ml_dtypes.float8_e4m3fn).astype(np.float64) * np.repeat(np.exp2(scales.astype(np.float64) - 127.0), 8, axis=1)[..., None]
    return vals.transpose(0, 1, 3, 2).reshape(g * 512, n)


E2M1 = np.array([0.0, 0.5, 1.0, 1.5, 2.0, 3.0, 4.0, 6.0, -0.0, -0.5, -1.0, -1.5, -2.0, -3.0, -4.0, -6.0])


def pack_fp4(w):
    k, n = w.shape
    w = f64(np.asarray(w, np.float32).astype(ml_dtypes.bfloat16)).reshape(k // 32, 32, n)
    amax = np.abs(w).max(1)
    mant, ex = np.frexp(amax / 6.0)
    byte = np.clip(np.where(amax > 0, np.where(mant > 0.5, ex, ex - 1) + 127, 1), 1, 254)
    scaled = (w * np.exp2(127.0 - byte)[:, None, :]).reshape(k, n).astype(np.float32)
    c = np.ascontiguousarray(scaled.reshape(k // 512, 128, 4, n).transpose(0, 1, 3, 2)).astype(ml_dtypes.float4_e2m1fn).view(np.uint8) & 0xF
    words = (c[..., 0::2] | (c[..., 1::2] << 4)).reshape(k // 512, 128, 2 * n)
    return np.ascontiguousarray(words), np.ascontiguousarray(byte.astype(np.uint8).reshape(k // 512, 16, n))


def unpack_fp4(words, scales):
    g, _, n = scales.shape
    words = np.ascontiguousarray(words).reshape(g, 128, n, 2)
    nib = np.empty((g, 128, n, 4), np.uint8)
    nib[..., 0::2] = words & 0xF
    nib[..., 1::2] = words >> 4
    vals = E2M1[nib] * np.repeat(np.exp2(scales.astype(np.float64) - 127.0), 8, axis=1)[..., None]
    return vals.transpose(0, 1, 3, 2).reshape(g * 512, n)


def planes(y):
    n, m = y.shape
    v = y.astype(np.float32).astype(ml_dtypes.bfloat16).astype(np.float64).reshape(n // 32, 32, m)
    top = np.abs(v).max(1)
    byte = np.clip(np.where(top > 0, np.frexp(top)[1] - 1 + 127 - 7, 1), 1, 254)
    codes = (v * np.exp2(127.0 - byte)[:, None, :]).reshape(n, m).astype(np.float32).astype(ml_dtypes.float8_e4m3fn).view(np.uint8)
    words = codes.reshape(n // 512, 128, 4, m).transpose(0, 1, 3, 2)
    return np.ascontiguousarray(words), np.ascontiguousarray(byte.astype(np.uint8).reshape(n // 512, 16, m))


K, T, S, N, H, J = 512, 2048, 512, 512, 512, 512


def setup_inputs():
    n = np.random.standard_normal
    s = mx_kscale(K)[:, None]
    u = mx_kscale(H)
    packed_xT = pack_weight(n((K, T)) * s)
    packed_w1 = pack_fp4(n((K, H)) / np.sqrt(K) / s)
    packed_w2 = pack_fp4(n((H, N)) / np.sqrt(H) / u[:, None])
    return {
        "x_words": packed_xT[0],
        "x_scales": packed_xT[1],
        "w1_words": packed_w1[0],
        "w1_scales": packed_w1[1],
        "tab": n((H, J)).astype(np.float32),
        "gn": (np.random.uniform(0.5, 1.5, (H, 1)) * u[:, None]).astype(np.float32),
        "w2_words": packed_w2[0],
        "w2_scales": packed_w2[1],
        "offs": striped(np.random.permutation(T)[:S]),
        "n1": striped8(np.random.randint(0, J, (8, S))),
        "n2": striped8(np.stack([np.random.permutation(S) for _ in range(8)])),
        "n3": striped8(np.stack([np.random.permutation(S) for _ in range(8)])),
        "n4": striped8(np.stack([np.random.permutation(S) for _ in range(8)])),
    }


def reference(x_words, x_scales, w1_words, w1_scales, tab, gn, w2_words, w2_scales, offs, n1, n2, n3, n4):
    xq = unpack_weight(x_words, x_scales)[:, unstriped(offs)]
    y = unpack_fp4(w1_words, w1_scales).T @ xq
    z = f64(gn) * (np.maximum(y + f64(tab)[np.arange(H)[:, None], runs(n1, H)], y[np.arange(H)[:, None], runs(n2, H)]))
    h = unpack_fp4(w2_words, w2_scales).T @ mxq(z, 0, "e4m3")
    st = h - (h[np.arange(N)[:, None], runs(n3, N)])
    out_0 = np.maximum(st, st[np.arange(N)[:, None], runs(n4, N)])
    return (out_0,) + planes(out_0)

@@ -1,0 +1,243 @@
+from contextlib import ExitStack
+
+import concourse.mybir as mybir
+
+F32 = mybir.dt.float32
+BF16 = mybir.dt.bfloat16
+I32 = mybir.dt.int32
+U32 = mybir.dt.uint32
+U16 = mybir.dt.uint16
+U8 = mybir.dt.uint8
+FP8X4 = mybir.dt.float8_e4m3fn_x4
+FP4X4 = mybir.dt.float4_e2m1fn_x4
+ALU = mybir.AluOpType
+COPY = mybir.ActivationFunctionType.Copy
+
+P = 128
+PACK = 4
+T = 2048
+S = 512
+LAST = PACK - 1
+PIECES = ((0, 256), (256, 384), (384, 512))
+EARLY_KINDS = 2
+FLOPS = 2 * 2 * 512 * 512 * 512
+
+
+def tile_picked_laykindhopmx_none_po_kernel(
+    tc, x_words, x_scales, w1_words, w1_scales, tab, gn, w2_words, w2_scales, offs, n1, n2, n3, n4, out_0, out_1, out_2
+):
+    nc = tc.nc
+    with ExitStack() as ctx:
+        pool = ctx.enter_context(tc.tile_pool(name="held", bufs=1))
+        psum = ctx.enter_context(tc.psum_pool(name="psum", bufs=1))
+
+        def sb(name, cols, dtype, tag=""):
+            return pool.tile([P, cols], dtype, name=name, align_bytes=64, tag=tag)
+
+        def load_list(name, src):
+            tile = pool.tile([P, S // 16], U16, name=name)
+            nc.sync.dma_start(tile[:], src)
+            return tile
+
+        def load_scale_rows(engine, tile, src):
+            for q in range(4):
+                engine.dma_start(tile[32 * q : 32 * q + 4, :].bitcast(I32), src[0, 4 * q : 4 * q + 4, :].bitcast(I32))
+
+        def deal_words(dealt, raw, t0, t1):
+            nc.vector.tensor_copy(
+                dealt.rearrange("p (t m b) -> p t m b", m=P, b=2), raw[:].rearrange("p (m t b) -> p t m b", t=PACK, b=2)[:, t0:t1]
+            )
+
+        def deal_scales(dealt, raw, t0, t1):
+            nc.vector.tensor_copy(dealt.rearrange("p (t m) -> p t m", m=P), raw[:].rearrange("p (m t) -> p t m", t=PACK)[:, t0:t1])
+
+        def look_up(win, offsets, lo, hi):
+            return win[:].indirect(offsets[:, lo // 16 : hi // 16])
+
+        xs_raw = sb("xs_raw", T, U8, tag="xs_then_w2")
+        ws_raw = sb("ws_raw", S, U8)
+        nc.vector.memset(xs_raw[:].bitcast(I32), 0)
+        nc.vector.memset(ws_raw[:].bitcast(I32), 0)
+
+        tab_rows = tab.rearrange("(p t) c -> p t c", t=PACK)
+
+        def load_tab(t, tag):
+            win = sb("tab_win" + str(t), 2 * S, F32, tag=tag)
+            nc.sync.dma_start(win[:, :S], tab_rows[:, t, :])
+            return win
+
+        offs_t = load_list("offs_t", offs)
+        n1_t = load_list("n1_t", n1)
+        w1w_raw = sb("w1w_raw", 2 * S, U8, tag="w1_then_gain")
+        nc.sync.dma_start(w1w_raw[:].bitcast(I32), w1_words[0].bitcast(I32))
+        tab_win = {0: load_tab(0, "tab")}
+        xw_raw = sb("xw_raw", T, U32, tag="xw_then_tab")
+        load_scale_rows(nc.sync, xs_raw, x_scales)
+        nc.sync.dma_start(xw_raw[:].bitcast(I32), x_words[0].rearrange("p c r -> p (c r)").bitcast(I32))
+        load_scale_rows(nc.sync, ws_raw, w1_scales)
+        n2_t = load_list("n2_t", n2)
+        n3_t = load_list("n3_t", n3)
+        n4_t = load_list("n4_t", n4)
+
+        kind = [sb("kind" + str(t), S, F32) for t in range(EARLY_KINDS)]
+
+        def fetch_kind(t):
+            nc.vector.tensor_copy(kind[t][:], look_up(tab_win[t], n1_t, 0, S))
+
+        w1w = sb("w1w", 2 * S, U8)
+        w1s = sb("w1s", S, U8)
+        deal_words(w1w[:], w1w_raw, 0, PACK)
+        gain = sb("gain", PACK, F32, tag="w1_then_gain")
+        nc.sync.dma_start(gain[:], gn.rearrange("(p t) o -> p (t o)", t=PACK))
+        fetch_kind(0)
+        tab_win[1] = load_tab(1, "tab")
+        xw = sb("xw", S, U32)
+        xs = sb("xs", S, U8)
+        nc.vector.tensor_copy(xs[:], xs_raw[:].indirect(offs_t[:]))
+        w2w_raw = sb("w2w_raw", 2 * S, U8, tag="xs_then_w2")
+        nc.sync.dma_start(w2w_raw[:].bitcast(I32), w2_words[0].bitcast(I32))
+        nc.vector.tensor_copy(xw[:], xw_raw[:].indirect(offs_t[:]))
+        tab_win[2] = load_tab(2, "xw_then_tab")
+        deal_scales(w1s[:], ws_raw, 0, PACK)
+        load_scale_rows(nc.sync, ws_raw, w2_scales)
+
+        def product(bank, words, scales, t, codes, code_scales, lo, hi):
+            nc.tensor.matmul_mx(
+                out=bank[:, lo:hi],
+                lhsT=words[:, 2 * P * t : 2 * P * (t + 1)].bitcast(FP4X4),
+                lhsT_scale=scales[:, P * t : P * (t + 1)],
+                rhs=codes[:, lo:hi].bitcast(FP8X4),
+                rhs_scale=code_scales[:, lo:hi],
+                start=True,
+                stop=True,
+            )
+
+        def window(name, t):
+            return sb(name + str(t), S if t == LAST else 2 * S, F32)
+
+        y_bank = [psum.tile([P, S], F32, name="y_bank" + str(t)) for t in range(PACK)]
+        y_win = [window("y_win", t) for t in range(PACK)]
+        for t in range(PACK):
+            product(y_bank[t], w1w, w1s, t, xw, xs, 0, S)
+            nc.scalar.activation(y_win[t][:, :S], y_bank[t][:], COPY)
+
+        first = [sb("first" + str(t), S, F32) for t in range(PACK)]
+        second = [sb("second" + str(t), S, F32) for t in range(PACK)]
+        larger = sb("larger", PACK * S, F32)
+        z_bf = [sb("z_bf" + str(i), PACK * (hi - lo), BF16) for i, (lo, hi) in enumerate(PIECES)]
+        z_codes = sb("z_codes", S, U32)
+        z_scales = sb("z_scales", S, U8)
+
+        def plane(tiles, i, t):
+            return tiles[i][:].rearrange("p (c t) -> p t c", t=PACK)[:, t, :]
+
+        def by_column(planes, lo, hi):
+            return planes[:].rearrange("p (t c) -> p c t", t=PACK)[:, lo:hi, :]
+
+        def quantize(codes, scales, tiles, i):
+            lo, hi = PIECES[i]
+            nc.vector.quantize_mx(out=codes[:, lo:hi].bitcast(FP8X4), scales=scales[:, lo:hi], in_=tiles[i][:])
+
+        def z_add(t):
+            if t < EARLY_KINDS:
+                nc.vector.tensor_tensor(first[t][:], kind[t][:], y_win[t][:, :S], ALU.add)
+            else:
+                nc.vector.tensor_tensor(first[t][:], look_up(tab_win[t], n1_t, 0, S), y_win[t][:, :S], ALU.add)
+
+        def z_fetch(t, lo, hi):
+            nc.vector.tensor_copy(second[t][:, lo:hi], look_up(y_win[t], n2_t, lo, hi))
+
+        def z_max(t, lo, hi):
+            nc.vector.tensor_tensor(larger[:, t * S + lo : t * S + hi], first[t][:, lo:hi], second[t][:, lo:hi], ALU.max)
+            for i, (a, b) in enumerate(PIECES[:2]):
+                if lo <= a and b <= hi:
+                    nc.scalar.activation(plane(z_bf, i, t), larger[:, t * S + a : t * S + b], COPY, scale=gain[:, t : t + 1])
+
+        fetch_kind(1)
+        tab_win[3] = load_tab(3, "tab")
+        w2w = sb("w2w", 2 * S, U8)
+        w2s = sb("w2s", S, U8)
+        deal_words(w2w[:, : 2 * P], w2w_raw, 0, 1)
+        deal_scales(w2s[:, :P], ws_raw, 0, 1)
+        z_add(0)
+        for t in range(LAST):
+            z_fetch(t, 0, S)
+            z_add(t + 1)
+            z_max(t, 0, S)
+        z_fetch(LAST, *PIECES[0])
+        z_fetch(LAST, *PIECES[1])
+        z_max(LAST, *PIECES[0])
+        z_fetch(LAST, *PIECES[2])
+        z_max(LAST, *PIECES[1])
+        z_max(LAST, *PIECES[2])
+        lo, hi = PIECES[2]
+        nc.vector.tensor_tensor(
+            z_bf[2][:].rearrange("p (c t) -> p c t", t=PACK),
+            by_column(larger, lo, hi),
+            gain[:].rearrange("p (o t) -> p o t", o=1).to_broadcast([P, hi - lo, PACK]),
+            ALU.mult,
+        )
+
+        h_bank = [psum.tile([P, S], F32, name="h_bank" + str(t)) for t in range(PACK)]
+        h_neg = [sb("h_neg" + str(t), 2 * S, F32) for t in range(PACK)]
+        h = [sb("h" + str(t), S, F32) for t in range(PACK)]
+
+        def layer2(t, lo, hi):
+            product(h_bank[t], w2w, w2s, t, z_codes, z_scales, lo, hi)
+            nc.scalar.activation(h_neg[t][:, lo:hi], h_bank[t][:, lo:hi], COPY, scale=-1.0)
+            nc.scalar.copy(h[t][:, lo:hi], h_bank[t][:, lo:hi])
+
+        for i, (lo, hi) in enumerate(PIECES):
+            quantize(z_codes, z_scales, z_bf, i)
+            layer2(0, lo, hi)
+        deal_words(w2w[:, 2 * P :], w2w_raw, 1, PACK)
+        deal_scales(w2s[:, P:], ws_raw, 1, PACK)
+        for t in range(1, PACK):
+            layer2(t, 0, S)
+
+        st_win = [window("st_win", t) for t in range(PACK)]
+        hop = [sb("hop" + str(t), S, F32) for t in range(PACK)]
+        result = sb("result", PACK * S, F32)
+        r_bf = [sb("r_bf" + str(i), PACK * (hi - lo), BF16) for i, (lo, hi) in enumerate(PIECES)]
+        r_codes = sb("r_codes", S, U32)
+        r_scales = sb("r_scales", S, U8)
+        out_rows = out_0.rearrange("(p t) c -> p t c", t=PACK)
+
+        def step(t):
+            nc.vector.tensor_tensor(st_win[t][:, :S], look_up(h_neg[t], n3_t, 0, S), h[t][:], ALU.add)
+
+        def fetch_hop(t, lo, hi):
+            nc.vector.tensor_copy(hop[t][:, lo:hi], look_up(st_win[t], n4_t, lo, hi))
+
+        def finish(t, lo, hi):
+            nc.vector.tensor_tensor(result[:, t * S + lo : t * S + hi], st_win[t][:, lo:hi], hop[t][:, lo:hi], ALU.max)
+            nc.sync.dma_start(out_rows[:, t, lo:hi], result[:, t * S + lo : t * S + hi])
+            for i, (a, b) in enumerate(PIECES[:2]):
+                if lo <= a and b <= hi:
+                    nc.scalar.copy(plane(r_bf, i, t), result[:, t * S + a : t * S + b])
+
+        step(0)
+        step(1)
+        fetch_hop(0, 0, S)
+        fetch_hop(1, 0, S)
+        finish(0, 0, S)
+        step(2)
+        finish(1, 0, S)
+        fetch_hop(2, 0, S)
+        step(3)
+        finish(2, 0, S)
+        fetch_hop(LAST, *PIECES[0])
+        fetch_hop(LAST, *PIECES[1])
+        finish(LAST, *PIECES[0])
+        fetch_hop(LAST, *PIECES[2])
+        finish(LAST, *PIECES[1])
+        finish(LAST, *PIECES[2])
+        lo, hi = PIECES[2]
+        nc.vector.tensor_copy(r_bf[2][:].rearrange("p (c t) -> p c t", t=PACK), by_column(result, lo, hi))
+        words_out = out_1[0].rearrange("p c r -> p (c r)").bitcast(I32)
+        for i, (lo, hi) in enumerate(PIECES):
+            quantize(r_codes, r_scales, r_bf, i)
+            nc.sync.dma_start(words_out[:, lo:hi], r_codes[:, lo:hi].bitcast(I32))
+        for q in range(4):
+            engine = nc.scalar if q % 2 else nc.sync
+            engine.dma_start(out_2[0, 4 * q : 4 * q + 4, :].bitcast(I32), r_scales[32 * q : 32 * q + 4, :].bitcast(I32))

@@ -19,7 +19,7 @@ T = 2048
 S = 512
 LAST = PACK - 1
 PIECES = ((0, 256), (256, 384), (384, 512))
-EARLY_KINDS = 2
+EARLY_KINDS = 1
 FLOPS = 2 * 2 * 512 * 512 * 512
 
 
@@ -54,28 +54,33 @@ def tile_picked_laykindhopmx_none_po_kernel(
         def look_up(win, offsets, lo, hi):
             return win[:].indirect(offsets[:, lo // 16 : hi // 16])
 
-        xs_raw = sb("xs_raw", T, U8, tag="xs_then_w2")
+        xs_raw = sb("xs_raw", T, U8)
         ws_raw = sb("ws_raw", S, U8)
         nc.vector.memset(xs_raw[:].bitcast(I32), 0)
         nc.vector.memset(ws_raw[:].bitcast(I32), 0)
 
         tab_rows = tab.rearrange("(p t) c -> p t c", t=PACK)
 
-        def load_tab(t, tag):
-            win = sb("tab_win" + str(t), 2 * S, F32, tag=tag)
+        def load_tab(t):
+            win = sb("tab_win" + str(t), 2 * S, F32)
             nc.sync.dma_start(win[:, :S], tab_rows[:, t, :])
             return win
 
         offs_t = load_list("offs_t", offs)
-        n1_t = load_list("n1_t", n1)
-        w1w_raw = sb("w1w_raw", 2 * S, U8, tag="w1_then_gain")
+        w1w_raw = sb("w1w_raw", 2 * S, U8)
         nc.sync.dma_start(w1w_raw[:].bitcast(I32), w1_words[0].bitcast(I32))
-        tab_win = {0: load_tab(0, "tab")}
-        xw_raw = sb("xw_raw", T, U32, tag="xw_then_tab")
+        w2w_raw = sb("w2w_raw", 2 * S, U8)
+        nc.sync.dma_start(w2w_raw[:].bitcast(I32), w2_words[0].bitcast(I32))
         load_scale_rows(nc.sync, xs_raw, x_scales)
+        xw_raw = sb("xw_raw", T, U32)
         nc.sync.dma_start(xw_raw[:].bitcast(I32), x_words[0].rearrange("p c r -> p (c r)").bitcast(I32))
         load_scale_rows(nc.sync, ws_raw, w1_scales)
+        n1_t = load_list("n1_t", n1)
+        tab_win = [load_tab(0), load_tab(1)]
         n2_t = load_list("n2_t", n2)
+        gain = sb("gain", PACK, F32)
+        nc.sync.dma_start(gain[:], gn.rearrange("(p t) o -> p (t o)", t=PACK))
+        tab_win.extend([load_tab(2), load_tab(3)])
         n3_t = load_list("n3_t", n3)
         n4_t = load_list("n4_t", n4)
 
@@ -87,17 +92,12 @@ def tile_picked_laykindhopmx_none_po_kernel(
         w1w = sb("w1w", 2 * S, U8)
         w1s = sb("w1s", S, U8)
         deal_words(w1w[:], w1w_raw, 0, PACK)
-        gain = sb("gain", PACK, F32, tag="w1_then_gain")
-        nc.sync.dma_start(gain[:], gn.rearrange("(p t) o -> p (t o)", t=PACK))
-        fetch_kind(0)
-        tab_win[1] = load_tab(1, "tab")
         xw = sb("xw", S, U32)
         xs = sb("xs", S, U8)
         nc.vector.tensor_copy(xs[:], xs_raw[:].indirect(offs_t[:]))
-        w2w_raw = sb("w2w_raw", 2 * S, U8, tag="xs_then_w2")
-        nc.sync.dma_start(w2w_raw[:].bitcast(I32), w2_words[0].bitcast(I32))
+        w2w_early = sb("w2w_early", S, U8)
+        deal_words(w2w_early[:], w2w_raw, 0, 2)
         nc.vector.tensor_copy(xw[:], xw_raw[:].indirect(offs_t[:]))
-        tab_win[2] = load_tab(2, "xw_then_tab")
         deal_scales(w1s[:], ws_raw, 0, PACK)
         load_scale_rows(nc.sync, ws_raw, w2_scales)
 
@@ -115,16 +115,16 @@ def tile_picked_laykindhopmx_none_po_kernel(
         def window(name, t):
             return sb(name + str(t), S if t == LAST else 2 * S, F32)
 
-        y_bank = [psum.tile([P, S], F32, name="y_bank" + str(t)) for t in range(PACK)]
+        y_bank = [psum.tile([P, S], F32, name="y_bank" + str(t), tag="bank" + str(t)) for t in range(PACK)]
         y_win = [window("y_win", t) for t in range(PACK)]
         for t in range(PACK):
             product(y_bank[t], w1w, w1s, t, xw, xs, 0, S)
             nc.scalar.activation(y_win[t][:, :S], y_bank[t][:], COPY)
 
         first = [sb("first" + str(t), S, F32) for t in range(PACK)]
-        second = [sb("second" + str(t), S, F32) for t in range(PACK)]
-        larger = sb("larger", PACK * S, F32)
-        z_bf = [sb("z_bf" + str(i), PACK * (hi - lo), BF16) for i, (lo, hi) in enumerate(PIECES)]
+        second = [sb("second" + str(t), S, F32, tag="second" + str(t)) for t in range(PACK)]
+        larger = sb("larger", PACK * S, F32, tag="larger")
+        z_bf = [sb("z_bf" + str(i), PACK * (hi - lo), BF16, tag="z_bf" + str(i)) for i, (lo, hi) in enumerate(PIECES)]
         z_codes = sb("z_codes", S, U32)
         z_scales = sb("z_scales", S, U8)
 
@@ -153,23 +153,32 @@ def tile_picked_laykindhopmx_none_po_kernel(
                 if lo <= a and b <= hi:
                     nc.scalar.activation(plane(z_bf, i, t), larger[:, t * S + a : t * S + b], COPY, scale=gain[:, t : t + 1])
 
-        fetch_kind(1)
-        tab_win[3] = load_tab(3, "tab")
-        w2w = sb("w2w", 2 * S, U8)
-        w2s = sb("w2s", S, U8)
-        deal_words(w2w[:, : 2 * P], w2w_raw, 0, 1)
-        deal_scales(w2s[:, :P], ws_raw, 0, 1)
+        fetch_kind(0)
         z_add(0)
-        for t in range(LAST):
+        for t in range(LAST - 1):
             z_fetch(t, 0, S)
             z_add(t + 1)
             z_max(t, 0, S)
+        z_fetch(LAST - 1, 0, S)
+        w2_early = (w2w_early, sb("w2s_early", S // 2, U8, tag="second1"))
+        deal_scales(w2_early[1][:], ws_raw, 0, 2)
+        z_max(LAST - 1, 0, S)
+        z_add(LAST)
         z_fetch(LAST, *PIECES[0])
         z_fetch(LAST, *PIECES[1])
         z_max(LAST, *PIECES[0])
         z_fetch(LAST, *PIECES[2])
         z_max(LAST, *PIECES[1])
         z_max(LAST, *PIECES[2])
+        h_neg = [sb("h_neg" + str(t), 2 * S, F32) for t in range(PACK)]
+        h = [sb("h" + str(t), S, F32) for t in range(PACK)]
+
+        def layer2(t, weights, lo, hi, bank_tag):
+            bank = psum.tile([P, S], F32, name="h_bank", tag=bank_tag)
+            product(bank, *weights, t % 2, z_codes, z_scales, lo, hi)
+            nc.scalar.activation(h_neg[t][:, lo:hi], bank[:, lo:hi], COPY, scale=-1.0)
+            nc.scalar.copy(h[t][:, lo:hi], bank[:, lo:hi])
+
         lo, hi = PIECES[2]
         nc.vector.tensor_tensor(
             z_bf[2][:].rearrange("p (c t) -> p c t", t=PACK),
@@ -177,23 +186,15 @@ def tile_picked_laykindhopmx_none_po_kernel(
             gain[:].rearrange("p (o t) -> p o t", o=1).to_broadcast([P, hi - lo, PACK]),
             ALU.mult,
         )
-
-        h_bank = [psum.tile([P, S], F32, name="h_bank" + str(t)) for t in range(PACK)]
-        h_neg = [sb("h_neg" + str(t), 2 * S, F32) for t in range(PACK)]
-        h = [sb("h" + str(t), S, F32) for t in range(PACK)]
-
-        def layer2(t, lo, hi):
-            product(h_bank[t], w2w, w2s, t, z_codes, z_scales, lo, hi)
-            nc.scalar.activation(h_neg[t][:, lo:hi], h_bank[t][:, lo:hi], COPY, scale=-1.0)
-            nc.scalar.copy(h[t][:, lo:hi], h_bank[t][:, lo:hi])
-
-        for i, (lo, hi) in enumerate(PIECES):
+        for i in (0, 2, 1):
             quantize(z_codes, z_scales, z_bf, i)
-            layer2(0, lo, hi)
-        deal_words(w2w[:, 2 * P :], w2w_raw, 1, PACK)
-        deal_scales(w2s[:, P:], ws_raw, 1, PACK)
-        for t in range(1, PACK):
-            layer2(t, 0, S)
+            layer2(0, w2_early, *PIECES[i], "bank" + str(i))
+        layer2(1, w2_early, 0, S, "bank3")
+        w2_late = (sb("w2w_late", S, U8, tag="larger"), sb("w2s_late", S // 2, U8, tag="z_bf1"))
+        deal_words(w2_late[0][:], w2w_raw, 2, PACK)
+        deal_scales(w2_late[1][:], ws_raw, 2, PACK)
+        layer2(2, w2_late, 0, S, "bank4")
+        layer2(3, w2_late, 0, S, "bank5")
 
         st_win = [window("st_win", t) for t in range(PACK)]
         hop = [sb("hop" + str(t), S, F32) for t in range(PACK)]
@@ -211,33 +212,40 @@ def tile_picked_laykindhopmx_none_po_kernel(
 
         def finish(t, lo, hi):
             nc.vector.tensor_tensor(result[:, t * S + lo : t * S + hi], st_win[t][:, lo:hi], hop[t][:, lo:hi], ALU.max)
-            nc.sync.dma_start(out_rows[:, t, lo:hi], result[:, t * S + lo : t * S + hi])
             for i, (a, b) in enumerate(PIECES[:2]):
-                if lo <= a and b <= hi:
-                    nc.scalar.copy(plane(r_bf, i, t), result[:, t * S + a : t * S + b])
+                if t % 2 == 1 and lo <= a and b <= hi:
+                    pair = slice(t - 1, t + 1)
+                    nc.scalar.copy(r_bf[i][:].rearrange("p (c t) -> p c t", t=PACK)[:, :, pair], by_column(result, a, b)[:, :, pair])
+
+        def store(t, lo, hi):
+            nc.sync.dma_start(out_rows[:, t, lo:hi], result[:, t * S + lo : t * S + hi])
+
+        words_out = out_1[0].rearrange("p c r -> p (c r)").bitcast(I32)
+
+        def store_words(lo, hi):
+            nc.sync.dma_start(words_out[:, lo:hi], r_codes[:, lo:hi].bitcast(I32))
 
         step(0)
-        step(1)
-        fetch_hop(0, 0, S)
-        fetch_hop(1, 0, S)
-        finish(0, 0, S)
-        step(2)
-        finish(1, 0, S)
-        fetch_hop(2, 0, S)
-        step(3)
-        finish(2, 0, S)
+        for t in range(LAST):
+            fetch_hop(t, 0, S)
+            step(t + 1)
+            finish(t, 0, S)
+            store(t, 0, S)
         fetch_hop(LAST, *PIECES[0])
         fetch_hop(LAST, *PIECES[1])
         finish(LAST, *PIECES[0])
+        store(LAST, *PIECES[0])
         fetch_hop(LAST, *PIECES[2])
         finish(LAST, *PIECES[1])
         finish(LAST, *PIECES[2])
+        store(LAST, PIECES[1][0], S)
         lo, hi = PIECES[2]
         nc.vector.tensor_copy(r_bf[2][:].rearrange("p (c t) -> p c t", t=PACK), by_column(result, lo, hi))
-        words_out = out_1[0].rearrange("p c r -> p (c r)").bitcast(I32)
-        for i, (lo, hi) in enumerate(PIECES):
-            quantize(r_codes, r_scales, r_bf, i)
-            nc.sync.dma_start(words_out[:, lo:hi], r_codes[:, lo:hi].bitcast(I32))
+        quantize(r_codes, r_scales, r_bf, 0)
+        store_words(*PIECES[0])
+        quantize(r_codes, r_scales, r_bf, 2)
+        quantize(r_codes, r_scales, r_bf, 1)
+        store_words(PIECES[1][0], S)
         for q in range(4):
             engine = nc.scalar if q % 2 else nc.sync
             engine.dma_start(out_2[0, 4 * q : 4 * q + 4, :].bitcast(I32), r_scales[32 * q : 32 * q + 4, :].bitcast(I32))

@@ -14,12 +14,15 @@ ALU = mybir.AluOpType
 COPY = mybir.ActivationFunctionType.Copy
 
 P = 128
-PACK = 4
+PLANES = 4
+LAST = PLANES - 1
 T = 2048
 S = 512
-LAST = PACK - 1
-PIECES = ((0, 256), (256, 384), (384, 512))
-EARLY_KINDS = 1
+QUADRANTS = 4
+PIECE = 128
+PIECES = [(lo, lo + PIECE) for lo in range(0, S, PIECE)]
+RANGES = [(0, 2 * PIECE)] + PIECES[2:]
+SCALAR_COLS = S - PIECE
 FLOPS = 2 * 2 * 512 * 512 * 512
 
 
@@ -34,218 +37,204 @@ def tile_picked_laykindhopmx_none_po_kernel(
         def sb(name, cols, dtype, tag=""):
             return pool.tile([P, cols], dtype, name=name, align_bytes=64, tag=tag)
 
+        def planes(name):
+            return [sb(name + str(t), S, F32, tag=name + str(t)) for t in range(PLANES)]
+
+        def windows(name, last_in_pieces):
+            return [sb(name + str(t), S if last_in_pieces and t == LAST else 2 * S, F32) for t in range(PLANES)]
+
+        def look_up(window, entries, lo=0, hi=S):
+            return window[:].indirect(entries[:, lo // 16 : hi // 16])
+
         def load_list(name, src):
-            tile = pool.tile([P, S // 16], U16, name=name)
-            nc.sync.dma_start(tile[:], src)
-            return tile
+            entries = pool.tile([P, S // 16], U16, name=name)
+            nc.sync.dma_start(entries[:], src)
+            return entries
 
-        def load_scale_rows(engine, tile, src):
-            for q in range(4):
-                engine.dma_start(tile[32 * q : 32 * q + 4, :].bitcast(I32), src[0, 4 * q : 4 * q + 4, :].bitcast(I32))
+        def load_weight_words(name, src):
+            raw = sb(name, 2 * S, U8)
+            nc.sync.dma_start(raw[:].bitcast(I32), src[0].bitcast(I32))
+            return raw
 
-        def deal_words(dealt, raw, t0, t1):
+        def load_scale_rows(raw, src):
+            for q in range(QUADRANTS):
+                nc.sync.dma_start(raw[32 * q : 32 * q + 4, :].bitcast(I32), src[0, 4 * q : 4 * q + 4, :].bitcast(I32))
+
+        def deal_words(name, raw, t0, t1, tag=""):
+            dealt = sb(name, 2 * P * (t1 - t0), U8, tag=tag)
             nc.vector.tensor_copy(
-                dealt.rearrange("p (t m b) -> p t m b", m=P, b=2), raw[:].rearrange("p (m t b) -> p t m b", t=PACK, b=2)[:, t0:t1]
+                dealt[:].rearrange("p (t m b) -> p t m b", m=P, b=2),
+                raw[:].rearrange("p (m t b) -> p t m b", t=PLANES, b=2)[:, t0:t1],
+            )
+            return {t: dealt[:, 2 * P * (t - t0) : 2 * P * (t - t0 + 1)] for t in range(t0, t1)}
+
+        def deal_scales(name, raw, t0, t1, tag=""):
+            dealt = sb(name, P * (t1 - t0), U8, tag=tag)
+            nc.vector.tensor_copy(
+                dealt[:].rearrange("p (t m) -> p t m", m=P), raw[:].rearrange("p (m t) -> p t m", t=PLANES)[:, t0:t1]
+            )
+            return {t: dealt[:, P * (t - t0) : P * (t - t0 + 1)] for t in range(t0, t1)}
+
+        def product(bank_tag, words, scales, codes, code_scales, lo, hi):
+            bank = psum.tile([P, S], F32, name="bank", tag=bank_tag)
+            nc.tensor.matmul_mx(
+                out=bank[:, lo:hi],
+                lhsT=words.bitcast(FP4X4),
+                lhsT_scale=scales,
+                rhs=codes[:, lo:hi].bitcast(FP8X4),
+                rhs_scale=code_scales[:, lo:hi],
+                start=True,
+                stop=True,
+            )
+            return bank[:, lo:hi]
+
+        def quantize(codes, scales, rounded, lo, hi):
+            nc.vector.quantize_mx(
+                out=codes[:, lo:hi].bitcast(FP8X4), scales=scales[:, lo:hi], in_=rounded[:, PLANES * lo : PLANES * hi]
             )
 
-        def deal_scales(dealt, raw, t0, t1):
-            nc.vector.tensor_copy(dealt.rearrange("p (t m) -> p t m", m=P), raw[:].rearrange("p (m t) -> p t m", t=PACK)[:, t0:t1])
+        def by_column(tile, pattern):
+            return tile[:].rearrange(pattern + " -> p c t", t=PLANES)
 
-        def look_up(win, offsets, lo, hi):
-            return win[:].indirect(offsets[:, lo // 16 : hi // 16])
+        def last_plane(fetch, finish):
+            fetch(LAST, *PIECES[0])
+            for i in range(1, len(PIECES)):
+                fetch(LAST, *PIECES[i])
+                finish(LAST, *PIECES[i - 1])
+            finish(LAST, *PIECES[-1])
 
         xs_raw = sb("xs_raw", T, U8)
         ws_raw = sb("ws_raw", S, U8)
         nc.vector.memset(xs_raw[:].bitcast(I32), 0)
         nc.vector.memset(ws_raw[:].bitcast(I32), 0)
 
-        tab_rows = tab.rearrange("(p t) c -> p t c", t=PACK)
-
-        def load_tab(t):
-            win = sb("tab_win" + str(t), 2 * S, F32)
-            nc.sync.dma_start(win[:, :S], tab_rows[:, t, :])
-            return win
-
+        tab_rows = tab.rearrange("(p t) c -> p t c", t=PLANES)
+        tab_win = windows("tab_win", False)
         offs_t = load_list("offs_t", offs)
-        w1w_raw = sb("w1w_raw", 2 * S, U8)
-        nc.sync.dma_start(w1w_raw[:].bitcast(I32), w1_words[0].bitcast(I32))
-        w2w_raw = sb("w2w_raw", 2 * S, U8)
-        nc.sync.dma_start(w2w_raw[:].bitcast(I32), w2_words[0].bitcast(I32))
-        load_scale_rows(nc.sync, xs_raw, x_scales)
+        w1w_raw = load_weight_words("w1w_raw", w1_words)
+        w2w_raw = load_weight_words("w2w_raw", w2_words)
+        load_scale_rows(xs_raw, x_scales)
         xw_raw = sb("xw_raw", T, U32)
         nc.sync.dma_start(xw_raw[:].bitcast(I32), x_words[0].rearrange("p c r -> p (c r)").bitcast(I32))
-        load_scale_rows(nc.sync, ws_raw, w1_scales)
+        load_scale_rows(ws_raw, w1_scales)
         n1_t = load_list("n1_t", n1)
-        tab_win = [load_tab(0), load_tab(1)]
+        for t in (0, 1):
+            nc.sync.dma_start(tab_win[t][:, :S], tab_rows[:, t, :])
         n2_t = load_list("n2_t", n2)
-        gain = sb("gain", PACK, F32)
-        nc.sync.dma_start(gain[:], gn.rearrange("(p t) o -> p (t o)", t=PACK))
-        tab_win.extend([load_tab(2), load_tab(3)])
+        gain = sb("gain", PLANES, F32)
+        nc.sync.dma_start(gain[:], gn.rearrange("(p t) o -> p (t o)", t=PLANES))
+        for t in (2, 3):
+            nc.sync.dma_start(tab_win[t][:, :S], tab_rows[:, t, :])
         n3_t = load_list("n3_t", n3)
         n4_t = load_list("n4_t", n4)
 
-        kind = [sb("kind" + str(t), S, F32) for t in range(EARLY_KINDS)]
-
-        def fetch_kind(t):
-            nc.vector.tensor_copy(kind[t][:], look_up(tab_win[t], n1_t, 0, S))
-
-        w1w = sb("w1w", 2 * S, U8)
-        w1s = sb("w1s", S, U8)
-        deal_words(w1w[:], w1w_raw, 0, PACK)
-        xw = sb("xw", S, U32)
         xs = sb("xs", S, U8)
-        nc.vector.tensor_copy(xs[:], xs_raw[:].indirect(offs_t[:]))
-        w2w_early = sb("w2w_early", S, U8)
-        deal_words(w2w_early[:], w2w_raw, 0, 2)
-        nc.vector.tensor_copy(xw[:], xw_raw[:].indirect(offs_t[:]))
-        deal_scales(w1s[:], ws_raw, 0, PACK)
-        load_scale_rows(nc.sync, ws_raw, w2_scales)
+        xw = sb("xw", S, U32)
+        w1w = deal_words("w1w", w1w_raw, 0, PLANES)
+        nc.vector.tensor_copy(xs[:], look_up(xs_raw, offs_t))
+        w2w = deal_words("w2w_early", w2w_raw, 0, 2)
+        nc.vector.tensor_copy(xw[:], look_up(xw_raw, offs_t))
+        w1s = deal_scales("w1s_first", ws_raw, 0, 1)
+        w1s.update(deal_scales("w1s_rest", ws_raw, 1, PLANES))
+        load_scale_rows(ws_raw, w2_scales)
 
-        def product(bank, words, scales, t, codes, code_scales, lo, hi):
-            nc.tensor.matmul_mx(
-                out=bank[:, lo:hi],
-                lhsT=words[:, 2 * P * t : 2 * P * (t + 1)].bitcast(FP4X4),
-                lhsT_scale=scales[:, P * t : P * (t + 1)],
-                rhs=codes[:, lo:hi].bitcast(FP8X4),
-                rhs_scale=code_scales[:, lo:hi],
-                start=True,
-                stop=True,
-            )
+        y_win = windows("y_win", True)
+        for t in range(PLANES):
+            nc.scalar.activation(y_win[t][:, :S], product("bank" + str(t), w1w[t], w1s[t], xw, xs, 0, S), COPY)
 
-        def window(name, t):
-            return sb(name + str(t), S if t == LAST else 2 * S, F32)
-
-        y_bank = [psum.tile([P, S], F32, name="y_bank" + str(t), tag="bank" + str(t)) for t in range(PACK)]
-        y_win = [window("y_win", t) for t in range(PACK)]
-        for t in range(PACK):
-            product(y_bank[t], w1w, w1s, t, xw, xs, 0, S)
-            nc.scalar.activation(y_win[t][:, :S], y_bank[t][:], COPY)
-
-        first = [sb("first" + str(t), S, F32) for t in range(PACK)]
-        second = [sb("second" + str(t), S, F32, tag="second" + str(t)) for t in range(PACK)]
-        larger = sb("larger", PACK * S, F32, tag="larger")
-        z_bf = [sb("z_bf" + str(i), PACK * (hi - lo), BF16, tag="z_bf" + str(i)) for i, (lo, hi) in enumerate(PIECES)]
+        first = planes("first")
+        second = planes("second")
+        larger = sb("larger", PLANES * S, F32)
+        z_bf = sb("z_bf", PLANES * S, BF16, tag="z_bf")
         z_codes = sb("z_codes", S, U32)
         z_scales = sb("z_scales", S, U8)
 
-        def plane(tiles, i, t):
-            return tiles[i][:].rearrange("p (c t) -> p t c", t=PACK)[:, t, :]
+        def z_first(t):
+            nc.vector.tensor_tensor(first[t][:], look_up(tab_win[t], n1_t), y_win[t][:, :S], ALU.add)
 
-        def by_column(planes, lo, hi):
-            return planes[:].rearrange("p (t c) -> p c t", t=PACK)[:, lo:hi, :]
-
-        def quantize(codes, scales, tiles, i):
-            lo, hi = PIECES[i]
-            nc.vector.quantize_mx(out=codes[:, lo:hi].bitcast(FP8X4), scales=scales[:, lo:hi], in_=tiles[i][:])
-
-        def z_add(t):
-            if t < EARLY_KINDS:
-                nc.vector.tensor_tensor(first[t][:], kind[t][:], y_win[t][:, :S], ALU.add)
-            else:
-                nc.vector.tensor_tensor(first[t][:], look_up(tab_win[t], n1_t, 0, S), y_win[t][:, :S], ALU.add)
-
-        def z_fetch(t, lo, hi):
+        def z_second(t, lo=0, hi=S):
             nc.vector.tensor_copy(second[t][:, lo:hi], look_up(y_win[t], n2_t, lo, hi))
 
-        def z_max(t, lo, hi):
+        def z_finish(t, lo=0, hi=S):
             nc.vector.tensor_tensor(larger[:, t * S + lo : t * S + hi], first[t][:, lo:hi], second[t][:, lo:hi], ALU.max)
-            for i, (a, b) in enumerate(PIECES[:2]):
-                if lo <= a and b <= hi:
-                    nc.scalar.activation(plane(z_bf, i, t), larger[:, t * S + a : t * S + b], COPY, scale=gain[:, t : t + 1])
+            end = min(hi, SCALAR_COLS)
+            if lo < end:
+                nc.scalar.activation(
+                    by_column(z_bf, "p (c t)")[:, lo:end, t], larger[:, t * S + lo : t * S + end], COPY, scale=gain[:, t : t + 1]
+                )
 
-        fetch_kind(0)
-        z_add(0)
-        for t in range(LAST - 1):
-            z_fetch(t, 0, S)
-            z_add(t + 1)
-            z_max(t, 0, S)
-        z_fetch(LAST - 1, 0, S)
-        w2_early = (w2w_early, sb("w2s_early", S // 2, U8, tag="second1"))
-        deal_scales(w2_early[1][:], ws_raw, 0, 2)
-        z_max(LAST - 1, 0, S)
-        z_add(LAST)
-        z_fetch(LAST, *PIECES[0])
-        z_fetch(LAST, *PIECES[1])
-        z_max(LAST, *PIECES[0])
-        z_fetch(LAST, *PIECES[2])
-        z_max(LAST, *PIECES[1])
-        z_max(LAST, *PIECES[2])
-        h_neg = [sb("h_neg" + str(t), 2 * S, F32) for t in range(PACK)]
-        h = [sb("h" + str(t), S, F32) for t in range(PACK)]
-
-        def layer2(t, weights, lo, hi, bank_tag):
-            bank = psum.tile([P, S], F32, name="h_bank", tag=bank_tag)
-            product(bank, *weights, t % 2, z_codes, z_scales, lo, hi)
-            nc.scalar.activation(h_neg[t][:, lo:hi], bank[:, lo:hi], COPY, scale=-1.0)
-            nc.scalar.copy(h[t][:, lo:hi], bank[:, lo:hi])
-
-        lo, hi = PIECES[2]
+        kind = sb("kind", S, F32)
+        nc.vector.tensor_copy(kind[:], look_up(tab_win[0], n1_t))
+        nc.vector.tensor_tensor(first[0][:], kind[:], y_win[0][:, :S], ALU.add)
+        for t in (0, 1):
+            z_second(t)
+            z_first(t + 1)
+            z_finish(t)
+        z_second(2)
+        w2s = deal_scales("w2s_early", ws_raw, 0, 2, tag="second1")
+        z_finish(2)
+        z_first(LAST)
+        last_plane(z_second, z_finish)
         nc.vector.tensor_tensor(
-            z_bf[2][:].rearrange("p (c t) -> p c t", t=PACK),
-            by_column(larger, lo, hi),
-            gain[:].rearrange("p (o t) -> p o t", o=1).to_broadcast([P, hi - lo, PACK]),
+            by_column(z_bf, "p (c t)")[:, SCALAR_COLS:, :],
+            by_column(larger, "p (t c)")[:, SCALAR_COLS:, :],
+            gain[:].rearrange("p (o t) -> p o t", o=1).to_broadcast([P, PIECE, PLANES]),
             ALU.mult,
         )
-        for i in (0, 2, 1):
-            quantize(z_codes, z_scales, z_bf, i)
-            layer2(0, w2_early, *PIECES[i], "bank" + str(i))
-        layer2(1, w2_early, 0, S, "bank3")
-        w2_late = (sb("w2w_late", S, U8, tag="larger"), sb("w2s_late", S // 2, U8, tag="z_bf1"))
-        deal_words(w2_late[0][:], w2w_raw, 2, PACK)
-        deal_scales(w2_late[1][:], ws_raw, 2, PACK)
-        layer2(2, w2_late, 0, S, "bank4")
-        layer2(3, w2_late, 0, S, "bank5")
 
-        st_win = [window("st_win", t) for t in range(PACK)]
-        hop = [sb("hop" + str(t), S, F32) for t in range(PACK)]
-        result = sb("result", PACK * S, F32)
-        r_bf = [sb("r_bf" + str(i), PACK * (hi - lo), BF16) for i, (lo, hi) in enumerate(PIECES)]
+        h_neg = windows("h_neg", False)
+        h = planes("h")
+
+        def layer2(t, bank_tag, lo=0, hi=S):
+            sums = product(bank_tag, w2w[t], w2s[t], z_codes, z_scales, lo, hi)
+            nc.scalar.activation(h_neg[t][:, lo:hi], sums, COPY, scale=-1.0)
+            nc.scalar.copy(h[t][:, lo:hi], sums)
+
+        for i, (lo, hi) in enumerate(RANGES):
+            quantize(z_codes, z_scales, z_bf, lo, hi)
+            layer2(0, "bank" + str(i), lo, hi)
+        layer2(1, "bank3")
+        w2w.update(deal_words("w2w_late", w2w_raw, 2, PLANES, tag="z_bf"))
+        w2s.update(deal_scales("w2s_late", ws_raw, 2, PLANES, tag="second3"))
+        layer2(2, "bank4")
+        layer2(3, "bank5")
+
+        st_win = windows("st_win", True)
+        hop = planes("hop")
+        result = sb("result", PLANES * S, F32)
+        r_bf = sb("r_bf", PLANES * S, BF16)
         r_codes = sb("r_codes", S, U32)
         r_scales = sb("r_scales", S, U8)
-        out_rows = out_0.rearrange("(p t) c -> p t c", t=PACK)
+        out_rows = out_0.rearrange("(p t) c -> p t c", t=PLANES)
+        out_words = out_1[0].rearrange("p c r -> p (c r)").bitcast(I32)
 
         def step(t):
-            nc.vector.tensor_tensor(st_win[t][:, :S], look_up(h_neg[t], n3_t, 0, S), h[t][:], ALU.add)
+            nc.vector.tensor_tensor(st_win[t][:, :S], look_up(h_neg[t], n3_t), h[t][:], ALU.add)
 
-        def fetch_hop(t, lo, hi):
+        def fetch_hop(t, lo=0, hi=S):
             nc.vector.tensor_copy(hop[t][:, lo:hi], look_up(st_win[t], n4_t, lo, hi))
 
-        def finish(t, lo, hi):
+        def finish(t, lo=0, hi=S):
             nc.vector.tensor_tensor(result[:, t * S + lo : t * S + hi], st_win[t][:, lo:hi], hop[t][:, lo:hi], ALU.max)
-            for i, (a, b) in enumerate(PIECES[:2]):
-                if t % 2 == 1 and lo <= a and b <= hi:
-                    pair = slice(t - 1, t + 1)
-                    nc.scalar.copy(r_bf[i][:].rearrange("p (c t) -> p c t", t=PACK)[:, :, pair], by_column(result, a, b)[:, :, pair])
-
-        def store(t, lo, hi):
-            nc.sync.dma_start(out_rows[:, t, lo:hi], result[:, t * S + lo : t * S + hi])
-
-        words_out = out_1[0].rearrange("p c r -> p (c r)").bitcast(I32)
-
-        def store_words(lo, hi):
-            nc.sync.dma_start(words_out[:, lo:hi], r_codes[:, lo:hi].bitcast(I32))
+            if hi % (S // 2) == 0:
+                a = 0 if t < LAST else hi - S // 2
+                nc.sync.dma_start(out_rows[:, t, a:hi], result[:, t * S + a : t * S + hi])
+            end = min(hi, SCALAR_COLS)
+            if t % 2 == 1 and lo < end:
+                pair = slice(t - 1, t + 1)
+                nc.scalar.copy(by_column(r_bf, "p (c t)")[:, lo:end, pair], by_column(result, "p (t c)")[:, lo:end, pair])
 
         step(0)
         for t in range(LAST):
-            fetch_hop(t, 0, S)
+            fetch_hop(t)
             step(t + 1)
-            finish(t, 0, S)
-            store(t, 0, S)
-        fetch_hop(LAST, *PIECES[0])
-        fetch_hop(LAST, *PIECES[1])
-        finish(LAST, *PIECES[0])
-        store(LAST, *PIECES[0])
-        fetch_hop(LAST, *PIECES[2])
-        finish(LAST, *PIECES[1])
-        finish(LAST, *PIECES[2])
-        store(LAST, PIECES[1][0], S)
-        lo, hi = PIECES[2]
-        nc.vector.tensor_copy(r_bf[2][:].rearrange("p (c t) -> p c t", t=PACK), by_column(result, lo, hi))
-        quantize(r_codes, r_scales, r_bf, 0)
-        store_words(*PIECES[0])
-        quantize(r_codes, r_scales, r_bf, 2)
-        quantize(r_codes, r_scales, r_bf, 1)
-        store_words(PIECES[1][0], S)
-        for q in range(4):
-            engine = nc.scalar if q % 2 else nc.sync
-            engine.dma_start(out_2[0, 4 * q : 4 * q + 4, :].bitcast(I32), r_scales[32 * q : 32 * q + 4, :].bitcast(I32))
+            finish(t)
+        last_plane(fetch_hop, finish)
+        nc.vector.tensor_copy(by_column(r_bf, "p (c t)")[:, SCALAR_COLS:, :], by_column(result, "p (t c)")[:, SCALAR_COLS:, :])
+        for lo, hi in RANGES:
+            quantize(r_codes, r_scales, r_bf, lo, hi)
+        for lo, hi in ((0, S - PIECE), (S - PIECE, S)):
+            nc.sync.dma_start(out_words[:, lo:hi], r_codes[:, lo:hi].bitcast(I32))
+        for q in range(QUADRANTS):
+            queue = nc.scalar if q % 2 else nc.sync
+            queue.dma_start(out_2[0, 4 * q : 4 * q + 4, :].bitcast(I32), r_scales[32 * q : 32 * q + 4, :].bitcast(I32))

@@ -182,13 +182,11 @@ def tile_picked_laykindhopmx_none_po_kernel(
             ALU.mult,
         )
 
-        h_neg = windows("h_neg", False)
-        h = planes("h")
+        h_win = windows("h_win", False)
 
         def layer2(t, bank_tag, lo=0, hi=S):
             sums = product(bank_tag, w2w[t], w2s[t], z_codes, z_scales, lo, hi)
-            nc.scalar.activation(h_neg[t][:, lo:hi], sums, COPY, scale=-1.0)
-            nc.scalar.copy(h[t][:, lo:hi], sums)
+            nc.scalar.copy(h_win[t][:, lo:hi], sums)
 
         for i, (lo, hi) in enumerate(RANGES):
             quantize(z_codes, z_scales, z_bf, lo, hi)
@@ -200,7 +198,7 @@ def tile_picked_laykindhopmx_none_po_kernel(
         layer2(3, "bank5")
 
         st_win = windows("st_win", True)
-        hop = planes("hop")
+        hop = {}
         result = sb("result", PLANES * S, F32)
         r_bf = sb("r_bf", PLANES * S, BF16)
         r_codes = sb("r_codes", S, U32)
@@ -209,9 +207,13 @@ def tile_picked_laykindhopmx_none_po_kernel(
         out_words = out_1[0].rearrange("p c r -> p (c r)").bitcast(I32)
 
         def step(t):
-            nc.vector.tensor_tensor(st_win[t][:, :S], look_up(h_neg[t], n3_t), h[t][:], ALU.add)
+            far = pool.tile([P, S], F32, name="far", tag="far", bufs=2, align_bytes=64)
+            nc.vector.tensor_copy(far[:], look_up(h_win[t], n3_t))
+            nc.gpsimd.tensor_tensor(st_win[t][:, :S], h_win[t][:, :S], far[:], ALU.subtract)
 
         def fetch_hop(t, lo=0, hi=S):
+            if lo == 0:
+                hop[t] = pool.tile([P, S], F32, name="hop", tag="hop", bufs=2, align_bytes=64)
             nc.vector.tensor_copy(hop[t][:, lo:hi], look_up(st_win[t], n4_t, lo, hi))
 
         def finish(t, lo=0, hi=S):
@@ -225,9 +227,11 @@ def tile_picked_laykindhopmx_none_po_kernel(
                 nc.scalar.copy(by_column(r_bf, "p (c t)")[:, lo:end, pair], by_column(result, "p (t c)")[:, lo:end, pair])
 
         step(0)
+        step(1)
         for t in range(LAST):
             fetch_hop(t)
-            step(t + 1)
+            if t + 2 < PLANES:
+                step(t + 2)
             finish(t)
         last_plane(fetch_hop, finish)
         nc.vector.tensor_copy(by_column(r_bf, "p (c t)")[:, SCALAR_COLS:, :], by_column(result, "p (t c)")[:, SCALAR_COLS:, :])

from contextlib import ExitStack

import concourse.mybir as mybir

F32 = mybir.dt.float32
BF16 = mybir.dt.bfloat16
I32 = mybir.dt.int32
U32 = mybir.dt.uint32
U16 = mybir.dt.uint16
U8 = mybir.dt.uint8
FP8X4 = mybir.dt.float8_e4m3fn_x4
FP4X4 = mybir.dt.float4_e2m1fn_x4
ALU = mybir.AluOpType
COPY = mybir.ActivationFunctionType.Copy

P = 128
PLANES = 4
LAST = PLANES - 1
T = 2048
S = 512
QUADRANTS = 4
PIECE = 128
PIECES = [(lo, lo + PIECE) for lo in range(0, S, PIECE)]
RANGES = [(0, 2 * PIECE)] + PIECES[2:]
SCALAR_COLS = S - PIECE
FLOPS = 2 * 2 * 512 * 512 * 512


def tile_picked_laykindhopmx_none_po_kernel(
    tc, x_words, x_scales, w1_words, w1_scales, tab, gn, w2_words, w2_scales, offs, n1, n2, n3, n4, out_0, out_1, out_2
):
    nc = tc.nc
    with ExitStack() as ctx:
        pool = ctx.enter_context(tc.tile_pool(name="held", bufs=1))
        psum = ctx.enter_context(tc.psum_pool(name="psum", bufs=1))

        def sb(name, cols, dtype, tag=""):
            return pool.tile([P, cols], dtype, name=name, align_bytes=64, tag=tag)

        def planes(name):
            return [sb(name + str(t), S, F32, tag=name + str(t)) for t in range(PLANES)]

        def windows(name, last_in_pieces):
            return [sb(name + str(t), S if last_in_pieces and t == LAST else 2 * S, F32) for t in range(PLANES)]

        def look_up(window, entries, lo=0, hi=S):
            return window[:].indirect(entries[:, lo // 16 : hi // 16])

        def load_list(name, src):
            entries = pool.tile([P, S // 16], U16, name=name)
            nc.sync.dma_start(entries[:], src)
            return entries

        def load_weight_words(name, src):
            raw = sb(name, 2 * S, U8)
            nc.sync.dma_start(raw[:].bitcast(I32), src[0].bitcast(I32))
            return raw

        def load_scale_rows(raw, src):
            for q in range(QUADRANTS):
                nc.sync.dma_start(raw[32 * q : 32 * q + 4, :].bitcast(I32), src[0, 4 * q : 4 * q + 4, :].bitcast(I32))

        def deal_words(name, raw, t0, t1, tag=""):
            dealt = sb(name, 2 * P * (t1 - t0), U8, tag=tag)
            nc.vector.tensor_copy(
                dealt[:].rearrange("p (t m b) -> p t m b", m=P, b=2),
                raw[:].rearrange("p (m t b) -> p t m b", t=PLANES, b=2)[:, t0:t1],
            )
            return {t: dealt[:, 2 * P * (t - t0) : 2 * P * (t - t0 + 1)] for t in range(t0, t1)}

        def deal_scales(name, raw, t0, t1, tag=""):
            dealt = sb(name, P * (t1 - t0), U8, tag=tag)
            nc.vector.tensor_copy(
                dealt[:].rearrange("p (t m) -> p t m", m=P), raw[:].rearrange("p (m t) -> p t m", t=PLANES)[:, t0:t1]
            )
            return {t: dealt[:, P * (t - t0) : P * (t - t0 + 1)] for t in range(t0, t1)}

        def product(bank_tag, words, scales, codes, code_scales, lo, hi):
            bank = psum.tile([P, S], F32, name="bank", tag=bank_tag)
            nc.tensor.matmul_mx(
                out=bank[:, lo:hi],
                lhsT=words.bitcast(FP4X4),
                lhsT_scale=scales,
                rhs=codes[:, lo:hi].bitcast(FP8X4),
                rhs_scale=code_scales[:, lo:hi],
                start=True,
                stop=True,
            )
            return bank[:, lo:hi]

        def quantize(codes, scales, rounded, lo, hi):
            nc.vector.quantize_mx(
                out=codes[:, lo:hi].bitcast(FP8X4), scales=scales[:, lo:hi], in_=rounded[:, PLANES * lo : PLANES * hi]
            )

        def by_column(tile, pattern):
            return tile[:].rearrange(pattern + " -> p c t", t=PLANES)

        def last_plane(fetch, finish):
            fetch(LAST, *PIECES[0])
            for i in range(1, len(PIECES)):
                fetch(LAST, *PIECES[i])
                finish(LAST, *PIECES[i - 1])
            finish(LAST, *PIECES[-1])

        xs_raw = sb("xs_raw", T, U8)
        ws_raw = sb("ws_raw", S, U8)
        nc.vector.memset(xs_raw[:].bitcast(I32), 0)
        nc.vector.memset(ws_raw[:].bitcast(I32), 0)

        tab_rows = tab.rearrange("(p t) c -> p t c", t=PLANES)
        tab_win = windows("tab_win", False)
        offs_t = load_list("offs_t", offs)
        w1w_raw = load_weight_words("w1w_raw", w1_words)
        w2w_raw = load_weight_words("w2w_raw", w2_words)
        load_scale_rows(xs_raw, x_scales)
        xw_raw = sb("xw_raw", T, U32)
        nc.sync.dma_start(xw_raw[:].bitcast(I32), x_words[0].rearrange("p c r -> p (c r)").bitcast(I32))
        load_scale_rows(ws_raw, w1_scales)
        n1_t = load_list("n1_t", n1)
        for t in (0, 1):
            nc.sync.dma_start(tab_win[t][:, :S], tab_rows[:, t, :])
        n2_t = load_list("n2_t", n2)
        gain = sb("gain", PLANES, F32)
        nc.sync.dma_start(gain[:], gn.rearrange("(p t) o -> p (t o)", t=PLANES))
        for t in (2, 3):
            nc.sync.dma_start(tab_win[t][:, :S], tab_rows[:, t, :])
        n3_t = load_list("n3_t", n3)
        n4_t = load_list("n4_t", n4)

        xs = sb("xs", S, U8)
        xw = sb("xw", S, U32)
        w1w = deal_words("w1w", w1w_raw, 0, PLANES)
        nc.vector.tensor_copy(xs[:], look_up(xs_raw, offs_t))
        w2w = deal_words("w2w_early", w2w_raw, 0, 2)
        nc.vector.tensor_copy(xw[:], look_up(xw_raw, offs_t))
        w1s = deal_scales("w1s_first", ws_raw, 0, 1)
        w1s.update(deal_scales("w1s_rest", ws_raw, 1, PLANES))
        load_scale_rows(ws_raw, w2_scales)

        y_win = windows("y_win", True)
        for t in range(PLANES):
            nc.scalar.activation(y_win[t][:, :S], product("bank" + str(t), w1w[t], w1s[t], xw, xs, 0, S), COPY)

        first = planes("first")
        second = planes("second")
        larger = sb("larger", PLANES * S, F32)
        z_bf = sb("z_bf", PLANES * S, BF16, tag="z_bf")
        z_codes = sb("z_codes", S, U32)
        z_scales = sb("z_scales", S, U8)

        def z_first(t):
            nc.vector.tensor_tensor(first[t][:], look_up(tab_win[t], n1_t), y_win[t][:, :S], ALU.add)

        def z_second(t, lo=0, hi=S):
            nc.vector.tensor_copy(second[t][:, lo:hi], look_up(y_win[t], n2_t, lo, hi))

        def z_finish(t, lo=0, hi=S):
            nc.vector.tensor_tensor(larger[:, t * S + lo : t * S + hi], first[t][:, lo:hi], second[t][:, lo:hi], ALU.max)
            end = min(hi, SCALAR_COLS)
            if lo < end:
                nc.scalar.activation(
                    by_column(z_bf, "p (c t)")[:, lo:end, t], larger[:, t * S + lo : t * S + end], COPY, scale=gain[:, t : t + 1]
                )

        kind = sb("kind", S, F32)
        nc.vector.tensor_copy(kind[:], look_up(tab_win[0], n1_t))
        nc.vector.tensor_tensor(first[0][:], kind[:], y_win[0][:, :S], ALU.add)
        for t in (0, 1):
            z_second(t)
            z_first(t + 1)
            z_finish(t)
        z_second(2)
        w2s = deal_scales("w2s_early", ws_raw, 0, 2, tag="second1")
        z_finish(2)
        z_first(LAST)
        last_plane(z_second, z_finish)
        nc.vector.tensor_tensor(
            by_column(z_bf, "p (c t)")[:, SCALAR_COLS:, :],
            by_column(larger, "p (t c)")[:, SCALAR_COLS:, :],
            gain[:].rearrange("p (o t) -> p o t", o=1).to_broadcast([P, PIECE, PLANES]),
            ALU.mult,
        )

        h_win = windows("h_win", False)

        def layer2(t, bank_tag, lo=0, hi=S):
            sums = product(bank_tag, w2w[t], w2s[t], z_codes, z_scales, lo, hi)
            nc.scalar.copy(h_win[t][:, lo:hi], sums)

        for i, (lo, hi) in enumerate(RANGES):
            quantize(z_codes, z_scales, z_bf, lo, hi)
            layer2(0, "bank" + str(i), lo, hi)
        layer2(1, "bank3")
        w2w.update(deal_words("w2w_late", w2w_raw, 2, PLANES, tag="z_bf"))
        w2s.update(deal_scales("w2s_late", ws_raw, 2, PLANES, tag="second3"))
        layer2(2, "bank4")
        layer2(3, "bank5")

        st_win = windows("st_win", True)
        hop = {}
        result = sb("result", PLANES * S, F32)
        r_bf = sb("r_bf", PLANES * S, BF16)
        r_codes = sb("r_codes", S, U32)
        r_scales = sb("r_scales", S, U8)
        out_rows = out_0.rearrange("(p t) c -> p t c", t=PLANES)
        out_words = out_1[0].rearrange("p c r -> p (c r)").bitcast(I32)

        def step(t):
            far = pool.tile([P, S], F32, name="far", tag="far", bufs=2, align_bytes=64)
            nc.vector.tensor_copy(far[:], look_up(h_win[t], n3_t))
            nc.gpsimd.tensor_tensor(st_win[t][:, :S], h_win[t][:, :S], far[:], ALU.subtract)

        def fetch_hop(t, lo=0, hi=S):
            if lo == 0:
                hop[t] = pool.tile([P, S], F32, name="hop", tag="hop", bufs=2, align_bytes=64)
            nc.vector.tensor_copy(hop[t][:, lo:hi], look_up(st_win[t], n4_t, lo, hi))

        def finish(t, lo=0, hi=S):
            nc.vector.tensor_tensor(result[:, t * S + lo : t * S + hi], st_win[t][:, lo:hi], hop[t][:, lo:hi], ALU.max)
            if hi % (S // 2) == 0:
                a = 0 if t < LAST else hi - S // 2
                nc.sync.dma_start(out_rows[:, t, a:hi], result[:, t * S + a : t * S + hi])
            end = min(hi, SCALAR_COLS)
            if t % 2 == 1 and lo < end:
                pair = slice(t - 1, t + 1)
                nc.scalar.copy(by_column(r_bf, "p (c t)")[:, lo:end, pair], by_column(result, "p (t c)")[:, lo:end, pair])

        step(0)
        step(1)
        for t in range(LAST):
            fetch_hop(t)
            if t + 2 < PLANES:
                step(t + 2)
            finish(t)
        last_plane(fetch_hop, finish)
        nc.vector.tensor_copy(by_column(r_bf, "p (c t)")[:, SCALAR_COLS:, :], by_column(result, "p (t c)")[:, SCALAR_COLS:, :])
        for lo, hi in RANGES:
            quantize(r_codes, r_scales, r_bf, lo, hi)
        for lo, hi in ((0, S - PIECE), (S - PIECE, S)):
            nc.sync.dma_start(out_words[:, lo:hi], r_codes[:, lo:hi].bitcast(I32))
        for q in range(QUADRANTS):
            queue = nc.scalar if q % 2 else nc.sync
            queue.dma_start(out_2[0, 4 * q : 4 * q + 4, :].bitcast(I32), r_scales[32 * q : 32 * q + 4, :].bitcast(I32))
